import numpy as np
import ml_dtypes


def mxq(x, axis, fmt="e4m3"):
    dtype, down = {"e4m3": (ml_dtypes.float8_e4m3fn, 7), "e5m2": (ml_dtypes.float8_e5m2, 14)}[fmt]
    v = np.moveaxis(np.asarray(x, np.float32).astype(ml_dtypes.bfloat16).astype(np.float64), axis, -1)
    blocks = v.reshape(v.shape[:-1] + (-1, 32))
    amax = np.abs(blocks).max(-1, keepdims=True)
    byte = np.maximum(np.where(amax > 0, np.frexp(amax)[1] - 1 + 127, 0) - down, 1)
    scale = np.exp2(byte - 127.0)
    codes = (blocks / scale).astype(np.float32).astype(dtype).astype(np.float64)
    return np.moveaxis((codes * scale).reshape(v.shape), -1, axis)


WIDE = False


def mx_kscale(k):
    if not WIDE:
        return np.ones(k)
    levels = np.array([10, -10, 5, -5, 0])
    if k % 512:
        return np.exp2(np.random.permutation(np.resize(levels, k // 32))).repeat(32)
    a = np.empty((k // 512, 16))
    for p in range(k // 512):
        a[p, :8] = np.random.permutation(np.resize(levels, 8))
        for g in range(8):
            far = levels[np.abs(levels - a[p, g]) >= 10]
            a[p, g + 8] = far[np.random.randint(len(far))]
    return np.exp2(a.ravel()).repeat(32)


def f64(x):
    return np.asarray(x).astype(np.float64)


def striped(idx):
    return np.tile(idx.reshape(-1, 16).T, (8, 1)).astype(np.uint16)


def unstriped(offs):
    return offs[:16].T.reshape(-1).astype(np.int64)


def striped8(idx):
    return np.concatenate([x.reshape(-1, 16).T for x in idx]).astype(np.uint16)


def runs(offs, k):
    lists = np.stack([offs[16 * r : 16 * r + 16].T.reshape(-1) for r in range(8)]).astype(np.int64)
    return lists[np.arange(k) % 512 // 64]


def pack_weight(w):
    k, n = w.shape
    w = f64(np.asarray(w, np.float32).astype(ml_dtypes.bfloat16)).reshape(k // 32, 32, n)
    amax = np.abs(w).max(1)
    byte = np.clip(np.where(amax > 0, np.frexp(amax)[1] - 1 + 127 - 7, 1), 1, 254)
    scaled = (w * np.exp2(127.0 - byte)[:, None, :]).reshape(k, n).astype(np.float32)
    words = np.ascontiguousarray(scaled.reshape(k // 512, 128, 4, n).transpose(0, 1, 3, 2)).astype(ml_dtypes.float8_e4m3fn).view(np.uint8)
    return words, np.ascontiguousarray(byte.astype(np.uint8).reshape(k // 512, 16, n))


def unpack_weight(words, scales):
    g, p, n, _ = words.shape
    vals = np.ascontiguousarray(words).view(ml_dtypes.float8_e4m3fn).astype(np.float64) * np.repeat(np.exp2(scales.astype(np.float64) - 127.0), 8, axis=1)[..., None]
    return vals.transpose(0, 1, 3, 2).reshape(g * 512, n)


def sigmoid(v):
    return 1.0 / (1.0 + np.exp(-np.maximum(v, -700.0)))


K, T, S, N, H, W = 512, 2048, 512, 512, 512, 256


def setup_inputs():
    n = np.random.standard_normal
    s = mx_kscale(K)[:, None]
    u = mx_kscale(H)
    packed_xT = pack_weight(n((K, T)) * s)
    perm = np.stack([np.random.permutation(S) for _ in range(8)])
    return {
        "x_words": packed_xT[0],
        "x_scales": packed_xT[1],
        "w1": (n((K, H)) / np.sqrt(K) / s).astype(np.float32),
        "gn": (np.random.uniform(0.5, 1.5, (H, 1)) * u[:, None]).astype(np.float32),
        "gm": (np.random.uniform(0.5, 1.5, (H, 1)) * u[:, None]).astype(np.float32),
        "w2": (n((H, N)) / np.sqrt(2 * H) / u[:, None]).astype(np.float32),
        "w3": (n((H, N)) / np.sqrt(2 * H) / u[:, None]).astype(np.float32),
        "offs": striped(np.random.permutation(T)[:S]),
        "n1": striped8(perm[:, :W]),
        "n2": striped8(perm[:, W:]),
        "n3": striped8(np.stack([np.random.permutation(S) for _ in range(8)])),
        "n4": striped8(np.stack([np.random.permutation(S) for _ in range(8)])),
        "n5": striped8(np.stack([np.random.permutation(S) for _ in range(8)])),
        "n6": striped8(np.stack([np.random.permutation(S) for _ in range(8)])),
    }


def reference(x_words, x_scales, w1, gn, gm, w2, w3, offs, n1, n2, n3, n4, n5, n6):
    xq = unpack_weight(x_words, x_scales)[:, unstriped(offs)]
    y = mxq(f64(w1), 0, "e4m3").T @ xq
    pa = y[np.arange(H)[:, None], runs(n1, H)]
    pb = y[np.arange(H)[:, None], runs(n2, H)]
    rb = pa - pb
    ra = 0.75 * (pa + pb)
    ds = np.zeros((H, S))
    ds[np.arange(H)[:, None], runs(n1, H)] = ra
    dt = ds.copy()
    dt[np.arange(H)[:, None], runs(n2, H)] = rb
    z = f64(gn) * dt
    st = y[np.arange(H)[:, None], runs(n3, H)] - y
    z2 = f64(gm) * (y * (sigmoid(st[np.arange(H)[:, None], runs(n4, H)])))
    h = mxq(f64(w2), 0, "e4m3").T @ mxq(z, 0, "e4m3") + mxq(f64(w3), 0, "e4m3").T @ mxq(z2, 0, "e4m3")
    return h * (sigmoid(h[np.arange(N)[:, None], runs(n5, N)] - (h[np.arange(N)[:, None], runs(n6, N)])))

@@ -1,0 +1,233 @@
+from contextlib import ExitStack
+
+import concourse.mybir as mybir
+
+F32 = mybir.dt.float32
+BF16 = mybir.dt.bfloat16
+I32 = mybir.dt.int32
+U32 = mybir.dt.uint32
+U16 = mybir.dt.uint16
+U8 = mybir.dt.uint8
+FP8X4 = mybir.dt.float8_e4m3fn_x4
+ADD = mybir.AluOpType.add
+MULT = mybir.AluOpType.mult
+SUB = mybir.AluOpType.subtract
+COPY = mybir.ActivationFunctionType.Copy
+SIGMOID = mybir.ActivationFunctionType.Sigmoid
+
+P = 128
+PACK = 4
+T = 2048
+S = 512
+HALF = 256
+WIN = 1024
+FLOPS = 3 * 2 * 512 * 512 * 512
+
+
+def tile_picked_joinhaarhopdcmp_none_p_kernel(
+    tc, x_words, x_scales, w1, gn, gm, w2, w3, offs, n1, n2, n3, n4, n5, n6, out
+):
+    nc = tc.nc
+    with ExitStack() as ctx:
+        keep = ctx.enter_context(tc.tile_pool(name="keep", bufs=1))
+        psum = ctx.enter_context(tc.psum_pool(name="psum", bufs=1))
+
+        def tile(name, shape, dtype):
+            return keep.tile(shape, dtype, name=name, align_bytes=64)
+
+        def load_list(name, src):
+            dst = tile(name, list(src.shape), U16)
+            nc.sync.dma_start(dst[:], src)
+            return dst
+
+        def load_weight(name, src):
+            dst = tile(name, [P, PACK, S], F32)
+            nc.sync.dma_start(dst[:], src.rearrange("(p j) c -> p j c", j=PACK))
+            return dst
+
+        def load_gain(name, src):
+            dst = tile(name, [P, PACK], F32)
+            nc.sync.dma_start(dst[:], src.rearrange("(p t) o -> p (t o)", t=PACK))
+            return dst
+
+        def deal_pair(name, raw, pair, copy):
+            dst = tile(name, [P, 2, P, PACK], BF16)
+            copy(
+                dst[:].rearrange("p t m j -> p m j t"),
+                raw[:].rearrange("p j (m t) -> p m j t", t=PACK)[:, :, :, 2 * pair : 2 * pair + 2],
+            )
+            return dst
+
+        def quantise(name, src, width):
+            codes = tile(name + "_codes", [P, width], U32)
+            scales = tile(name + "_scales", [P, width], U8)
+            nc.vector.quantize_mx(out=codes[:].bitcast(FP8X4), scales=scales[:], in_=src)
+            return codes, scales
+
+        def quantise_pair(name, dealt):
+            return quantise(name, dealt[:].rearrange("p t m j -> p (t m j)"), 2 * P)
+
+        def mx_pass(acc, weights, t, moving, start, stop):
+            cols = slice((t % 2) * P, (t % 2 + 1) * P)
+            nc.tensor.matmul_mx(
+                out=acc[:],
+                lhsT=weights[0][:, cols].bitcast(FP8X4),
+                lhsT_scale=weights[1][:, cols],
+                rhs=moving[0][:].bitcast(FP8X4),
+                rhs_scale=moving[1][:],
+                start=start,
+                stop=stop,
+            )
+
+        table_scales = tile("table_scales", [P, T], U8)
+        nc.vector.memset(table_scales[:].bitcast(I32), 0)
+        three_quarters = tile("three_quarters", [P, HALF], F32)
+        nc.vector.memset(three_quarters[:], 0.75)
+
+        table_words = tile("table_words", [P, T], U32)
+        nc.sync.dma_start(table_words[:].bitcast(I32), x_words[0].rearrange("p n t -> p (n t)").bitcast(I32))
+        w1_raw = load_weight("w1_raw", w1)
+        offs_t = load_list("offs_t", offs)
+        for q in range(4):
+            nc.scalar.dma_start(
+                table_scales[32 * q : 32 * q + 4, :].bitcast(I32), x_scales[0, 4 * q : 4 * q + 4, :].bitcast(I32)
+            )
+        warm = tile("warm", [P, 1], F32)
+        nc.scalar.activation(warm[:], three_quarters[:, 0:1], SIGMOID)
+        n2_t = load_list("n2_t", n2)
+        n1_t = load_list("n1_t", n1)
+        n3_t = load_list("n3_t", n3)
+        gm_t = load_gain("gm_t", gm)
+        n4_t = load_list("n4_t", n4)
+        gn_t = load_gain("gn_t", gn)
+        w3_raw = load_weight("w3_raw", w3)
+        w2_raw = load_weight("w2_raw", w2)
+        n5_t = load_list("n5_t", n5)
+        n6_t = load_list("n6_t", n6)
+
+        rows = [tile("rows%d" % t, [P, WIN], F32) for t in range(PACK)]
+        steps = [tile("steps%d" % t, [P, WIN], F32) for t in range(PACK)]
+        for t in range(PACK):
+            nc.vector.memset(rows[t][:, S:], 0.0)
+        for t in range(PACK):
+            nc.vector.memset(steps[t][:, S:], 0.0)
+
+        picked_scales = tile("picked_scales", [P, S], U8)
+        nc.vector.tensor_copy(picked_scales[:], table_scales[:].indirect(offs_t[:]))
+        picked_words = tile("picked_words", [P, S], U32)
+        nc.vector.tensor_copy(picked_words[:], table_words[:].indirect(offs_t[:]))
+        picked = (picked_words, picked_scales)
+
+        y_banks = [psum.tile([P, S], F32, name="y_bank%d" % t) for t in range(PACK)]
+        for pair in range(2):
+            dealt = deal_pair("w1_dealt%d" % pair, w1_raw, pair, nc.vector.tensor_copy)
+            w1_q = quantise_pair("w1_q%d" % pair, dealt)
+            for t in (2 * pair, 2 * pair + 1):
+                mx_pass(y_banks[t], w1_q, t, picked, True, True)
+
+        y_plain = [tile("y_plain%d" % t, [P, S], F32) for t in range(PACK)]
+        y_gained = tile("y_gained", [P, PACK, S], F32)
+        gates = tile("gates", [P, PACK, S], F32)
+        z_planes = tile("z_planes", [P, PACK, S], BF16)
+        pb = [tile("pb%d" % t, [P, HALF], F32) for t in range(PACK)]
+        pb_less = [tile("pb_less%d" % t, [P, HALF], F32) for t in range(PACK)]
+        both = [tile("both%d" % t, [P, HALF], F32) for t in range(PACK)]
+        dt = [tile("dt%d" % t, [P, S], F32) for t in range(PACK)]
+        dealt23 = {}
+
+        def leave_bank(t):
+            nc.scalar.copy(rows[t][:, :S], y_banks[t][:])
+            nc.scalar.copy(y_plain[t][:], y_banks[t][:])
+
+        def fetch_pb(t):
+            nc.vector.tensor_copy(pb[t][:], rows[t][:].indirect(n2_t[:]))
+            nc.scalar.activation(pb_less[t][:], pb[t][:], COPY, scale=-2.0)
+
+        def fetch_step(t):
+            nc.vector.tensor_tensor(steps[t][:, :S], rows[t][:].indirect(n3_t[:]), y_plain[t][:], SUB)
+            nc.scalar.activation(gates[:, t, :], steps[t][:].indirect(n4_t[:]), SIGMOID)
+            nc.scalar.activation(y_gained[:, t, :], y_banks[t][:], COPY, scale=gm_t[:, t : t + 1])
+
+        def fetch_both(t):
+            nc.vector.tensor_tensor(both[t][:], rows[t][:].indirect(n1_t[:]), pb[t][:], ADD)
+
+        def put_ra(t):
+            nc.vector.tensor_tensor(dt[t][:].indirect(n1_t[:]), both[t][:], three_quarters[:], MULT)
+
+        def put_rb(t):
+            nc.vector.tensor_tensor(dt[t][:].indirect(n2_t[:]), both[t][:], pb_less[t][:], ADD)
+            nc.scalar.activation(z_planes[:, t, :], dt[t][:], COPY, scale=gn_t[:, t : t + 1])
+
+        weight_pairs = [("w3", w3_raw, 0), ("w2", w2_raw, 0), ("w3", w3_raw, 1), ("w2", w2_raw, 1)]
+        leave_bank(0)
+        fetch_pb(0)
+        for t in range(PACK):
+            if t + 1 < PACK:
+                leave_bank(t + 1)
+            fetch_step(t)
+            if t > 0:
+                put_rb(t - 1)
+            fetch_both(t)
+            if t + 1 < PACK:
+                fetch_pb(t + 1)
+            put_ra(t)
+            name, raw, pair = weight_pairs[t]
+            dealt23[name, pair] = deal_pair("%s_dealt%d" % (name, pair), raw, pair, nc.scalar.copy)
+        w3_q = [quantise_pair("w3_q0", dealt23["w3", 0])]
+        put_rb(PACK - 1)
+
+        z2_in = tile("z2_in", [P, S, PACK], BF16)
+        nc.vector.tensor_tensor(
+            z2_in[:].rearrange("p (c i) t -> p c t i", i=2),
+            y_gained[:].rearrange("p t (c i) -> p c t i", i=2),
+            gates[:].rearrange("p t (c i) -> p c t i", i=2),
+            MULT,
+        )
+        z_in = tile("z_in", [P, S, PACK], BF16)
+        nc.scalar.copy(
+            z_in[:].rearrange("p (c i) t -> p c t i", i=4), z_planes[:].rearrange("p t (c i) -> p c t i", i=4)
+        )
+        w2_q = [quantise_pair("w2_q0", dealt23["w2", 0])]
+        z2_q = quantise("z2_q", z2_in[:].rearrange("p c t -> p (c t)"), S)
+        z_q = quantise("z_q", z_in[:].rearrange("p c t -> p (c t)"), S)
+        w3_q.append(quantise_pair("w3_q1", dealt23["w3", 1]))
+        w2_q.append(quantise_pair("w2_q1", dealt23["w2", 1]))
+
+        h_banks = [psum.tile([P, S], F32, name="h_bank%d" % t) for t in range(PACK)]
+        for pair in range(2):
+            for t in (2 * pair, 2 * pair + 1):
+                mx_pass(h_banks[t], w3_q[pair], t, z2_q, True, False)
+            for t in (2 * pair, 2 * pair + 1):
+                mx_pass(h_banks[t], w2_q[pair], t, z_q, False, True)
+
+        out_rows = out.rearrange("(p t) c -> p t c", t=PACK)
+        pieces = [(0, 0, S), (1, 0, S), (2, 0, S), (3, 0, HALF), (3, HALF, S)]
+        second = [tile("second%d" % u, [P, b - a], F32) for u, (t, a, b) in enumerate(pieces)]
+        diff = [tile("diff%d" % u, [P, b - a], F32) for u, (t, a, b) in enumerate(pieces)]
+        gate = [tile("gate%d" % u, [P, b - a], F32) for u, (t, a, b) in enumerate(pieces)]
+        result = [tile("result%d" % u, [P, b - a], F32) for u, (t, a, b) in enumerate(pieces)]
+
+        def fetch_second(u):
+            t, a, b = pieces[u]
+            nc.vector.tensor_copy(second[u][:], rows[t][:].indirect(n6_t[:, a // 16 : b // 16]))
+
+        def fetch_diff(u):
+            t, a, b = pieces[u]
+            nc.vector.tensor_tensor(diff[u][:], rows[t][:].indirect(n5_t[:, a // 16 : b // 16]), second[u][:], SUB)
+            nc.scalar.activation(gate[u][:], diff[u][:], SIGMOID)
+
+        def finish(u):
+            t, a, b = pieces[u]
+            nc.vector.tensor_tensor(result[u][:], h_banks[t][:, a:b], gate[u][:], MULT)
+            nc.sync.dma_start(out_rows[:, t, a:b], result[u][:])
+
+        for t in range(PACK):
+            nc.scalar.copy(rows[t][:, :S], h_banks[t][:])
+        fetch_second(0)
+        for u in range(len(pieces)):
+            if u + 1 < len(pieces):
+                fetch_second(u + 1)
+            fetch_diff(u)
+            if u > 0:
+                finish(u - 1)
+        finish(len(pieces) - 1)

@@ -20,7 +20,6 @@ PACK = 4
 T = 2048
 S = 512
 HALF = 256
-WIN = 1024
 FLOPS = 3 * 2 * 512 * 512 * 512
 
 
@@ -32,8 +31,14 @@ def tile_picked_joinhaarhopdcmp_none_p_kernel(
         keep = ctx.enter_context(tc.tile_pool(name="keep", bufs=1))
         psum = ctx.enter_context(tc.psum_pool(name="psum", bufs=1))
 
-        def tile(name, shape, dtype):
-            return keep.tile(shape, dtype, name=name, align_bytes=64)
+        def tile(name, shape, dtype, tag=None):
+            return keep.tile(shape, dtype, name=name, tag=tag or name, align_bytes=64)
+
+        def cols(half):
+            return slice(half * HALF, (half + 1) * HALF)
+
+        def entries(list_tile, half):
+            return list_tile[:, half * (HALF // 16) : (half + 1) * (HALF // 16)]
 
         def load_list(name, src):
             dst = tile(name, list(src.shape), U16)
@@ -50,44 +55,36 @@ def tile_picked_joinhaarhopdcmp_none_p_kernel(
             nc.sync.dma_start(dst[:], src.rearrange("(p t) o -> p (t o)", t=PACK))
             return dst
 
-        def deal_pair(name, raw, pair, copy):
-            dst = tile(name, [P, 2, P, PACK], BF16)
+        def deal_pair(dst, raw, pair, copy):
             copy(
-                dst[:].rearrange("p t m j -> p m j t"),
+                dst.rearrange("p (t m j) -> p m j t", t=2, j=PACK),
                 raw[:].rearrange("p j (m t) -> p m j t", t=PACK)[:, :, :, 2 * pair : 2 * pair + 2],
             )
-            return dst
 
-        def quantise(name, src, width):
-            codes = tile(name + "_codes", [P, width], U32)
-            scales = tile(name + "_scales", [P, width], U8)
-            nc.vector.quantize_mx(out=codes[:].bitcast(FP8X4), scales=scales[:], in_=src)
-            return codes, scales
-
-        def quantise_pair(name, dealt):
-            return quantise(name, dealt[:].rearrange("p t m j -> p (t m j)"), 2 * P)
-
-        def mx_pass(acc, weights, t, moving, start, stop):
-            cols = slice((t % 2) * P, (t % 2 + 1) * P)
+        def mx_pass(acc, w_codes, w_scales, block, codes, scales, half, start, stop):
+            w_cols = slice(block * P, (block + 1) * P)
             nc.tensor.matmul_mx(
                 out=acc[:],
-                lhsT=weights[0][:, cols].bitcast(FP8X4),
-                lhsT_scale=weights[1][:, cols],
-                rhs=moving[0][:].bitcast(FP8X4),
-                rhs_scale=moving[1][:],
+                lhsT=w_codes[:, w_cols].bitcast(FP8X4),
+                lhsT_scale=w_scales[:, w_cols],
+                rhs=codes[:, cols(half)].bitcast(FP8X4),
+                rhs_scale=scales[:, cols(half)],
                 start=start,
                 stop=stop,
             )
+
+        def bank(name, t, half):
+            return psum.tile([P, HALF], F32, name="%s%d_%d" % (name, t, half), tag="bank%d_%d" % (t, half))
 
         table_scales = tile("table_scales", [P, T], U8)
         nc.vector.memset(table_scales[:].bitcast(I32), 0)
         three_quarters = tile("three_quarters", [P, HALF], F32)
         nc.vector.memset(three_quarters[:], 0.75)
 
+        offs_t = load_list("offs_t", offs)
+        w1_raw = load_weight("w1_raw", w1)
         table_words = tile("table_words", [P, T], U32)
         nc.sync.dma_start(table_words[:].bitcast(I32), x_words[0].rearrange("p n t -> p (n t)").bitcast(I32))
-        w1_raw = load_weight("w1_raw", w1)
-        offs_t = load_list("offs_t", offs)
         for q in range(4):
             nc.scalar.dma_start(
                 table_scales[32 * q : 32 * q + 4, :].bitcast(I32), x_scales[0, 4 * q : 4 * q + 4, :].bitcast(I32)
@@ -97,34 +94,36 @@ def tile_picked_joinhaarhopdcmp_none_p_kernel(
         n2_t = load_list("n2_t", n2)
         n1_t = load_list("n1_t", n1)
         n3_t = load_list("n3_t", n3)
-        gm_t = load_gain("gm_t", gm)
         n4_t = load_list("n4_t", n4)
+        gm_t = load_gain("gm_t", gm)
         gn_t = load_gain("gn_t", gn)
         w3_raw = load_weight("w3_raw", w3)
         w2_raw = load_weight("w2_raw", w2)
         n5_t = load_list("n5_t", n5)
         n6_t = load_list("n6_t", n6)
 
-        rows = [tile("rows%d" % t, [P, WIN], F32) for t in range(PACK)]
-        steps = [tile("steps%d" % t, [P, WIN], F32) for t in range(PACK)]
-        for t in range(PACK):
-            nc.vector.memset(rows[t][:, S:], 0.0)
-        for t in range(PACK):
-            nc.vector.memset(steps[t][:, S:], 0.0)
-
         picked_scales = tile("picked_scales", [P, S], U8)
         nc.vector.tensor_copy(picked_scales[:], table_scales[:].indirect(offs_t[:]))
+        w1_codes = tile("w1_codes", [P, S], U32)
+        w1_scales = tile("w1_scales", [P, S], U8)
+        for pair, copy in enumerate((nc.vector.tensor_copy, nc.scalar.copy)):
+            dealt = tile("w1_dealt%d" % pair, [P, 2 * S], BF16)
+            deal_pair(dealt[:], w1_raw, pair, copy)
+            nc.vector.quantize_mx(
+                out=w1_codes[:, cols(pair)].bitcast(FP8X4), scales=w1_scales[:, cols(pair)], in_=dealt[:]
+            )
         picked_words = tile("picked_words", [P, S], U32)
-        nc.vector.tensor_copy(picked_words[:], table_words[:].indirect(offs_t[:]))
-        picked = (picked_words, picked_scales)
+        for half in range(2):
+            nc.vector.tensor_copy(picked_words[:, cols(half)], table_words[:].indirect(entries(offs_t, half)))
 
-        y_banks = [psum.tile([P, S], F32, name="y_bank%d" % t) for t in range(PACK)]
-        for pair in range(2):
-            dealt = deal_pair("w1_dealt%d" % pair, w1_raw, pair, nc.vector.tensor_copy)
-            w1_q = quantise_pair("w1_q%d" % pair, dealt)
-            for t in (2 * pair, 2 * pair + 1):
-                mx_pass(y_banks[t], w1_q, t, picked, True, True)
+        y_banks = {}
+        for t in range(PACK):
+            for half in range(2):
+                y_banks[t, half] = bank("y", t, half)
+                mx_pass(y_banks[t, half], w1_codes, w1_scales, t, picked_words, picked_scales, half, True, True)
 
+        rows = [tile("rows%d" % t, [P, S], F32) for t in range(PACK)]
+        steps = [tile("steps%d" % t, [P, S], F32) for t in range(PACK)]
         y_plain = [tile("y_plain%d" % t, [P, S], F32) for t in range(PACK)]
         y_gained = tile("y_gained", [P, PACK, S], F32)
         gates = tile("gates", [P, PACK, S], F32)
@@ -133,20 +132,26 @@ def tile_picked_joinhaarhopdcmp_none_p_kernel(
         pb_less = [tile("pb_less%d" % t, [P, HALF], F32) for t in range(PACK)]
         both = [tile("both%d" % t, [P, HALF], F32) for t in range(PACK)]
         dt = [tile("dt%d" % t, [P, S], F32) for t in range(PACK)]
-        dealt23 = {}
+        w23_dealt = [tile("w23_dealt%d" % pair, [P, 4 * S], BF16) for pair in range(2)]
 
-        def leave_bank(t):
-            nc.scalar.copy(rows[t][:, :S], y_banks[t][:])
-            nc.scalar.copy(y_plain[t][:], y_banks[t][:])
+        def leave_banks(t):
+            for half in range(2):
+                nc.scalar.copy(rows[t][:, cols(half)], y_banks[t, half][:])
+                nc.scalar.copy(y_plain[t][:, cols(half)], y_banks[t, half][:])
 
         def fetch_pb(t):
             nc.vector.tensor_copy(pb[t][:], rows[t][:].indirect(n2_t[:]))
             nc.scalar.activation(pb_less[t][:], pb[t][:], COPY, scale=-2.0)
 
-        def fetch_step(t):
-            nc.vector.tensor_tensor(steps[t][:, :S], rows[t][:].indirect(n3_t[:]), y_plain[t][:], SUB)
-            nc.scalar.activation(gates[:, t, :], steps[t][:].indirect(n4_t[:]), SIGMOID)
-            nc.scalar.activation(y_gained[:, t, :], y_banks[t][:], COPY, scale=gm_t[:, t : t + 1])
+        def fetch_step(t, half):
+            nc.vector.tensor_tensor(
+                steps[t][:, cols(half)], rows[t][:].indirect(entries(n3_t, half)), y_plain[t][:, cols(half)], SUB
+            )
+
+        def fetch_gates(t):
+            for half in range(2):
+                nc.scalar.activation(gates[:, t, cols(half)], steps[t][:].indirect(entries(n4_t, half)), SIGMOID)
+            nc.scalar.activation(y_gained[:, t, :], y_plain[t][:], COPY, scale=gm_t[:, t : t + 1])
 
         def fetch_both(t):
             nc.vector.tensor_tensor(both[t][:], rows[t][:].indirect(n1_t[:]), pb[t][:], ADD)
@@ -158,76 +163,86 @@ def tile_picked_joinhaarhopdcmp_none_p_kernel(
             nc.vector.tensor_tensor(dt[t][:].indirect(n2_t[:]), both[t][:], pb_less[t][:], ADD)
             nc.scalar.activation(z_planes[:, t, :], dt[t][:], COPY, scale=gn_t[:, t : t + 1])
 
-        weight_pairs = [("w3", w3_raw, 0), ("w2", w2_raw, 0), ("w3", w3_raw, 1), ("w2", w2_raw, 1)]
-        leave_bank(0)
+        leave_banks(0)
         fetch_pb(0)
         for t in range(PACK):
             if t + 1 < PACK:
-                leave_bank(t + 1)
-            fetch_step(t)
-            if t > 0:
-                put_rb(t - 1)
+                leave_banks(t + 1)
+            fetch_step(t, 0)
             fetch_both(t)
+            fetch_step(t, 1)
+            fetch_gates(t)
+            put_ra(t)
             if t + 1 < PACK:
                 fetch_pb(t + 1)
-            put_ra(t)
-            name, raw, pair = weight_pairs[t]
-            dealt23[name, pair] = deal_pair("%s_dealt%d" % (name, pair), raw, pair, nc.scalar.copy)
-        w3_q = [quantise_pair("w3_q0", dealt23["w3", 0])]
-        put_rb(PACK - 1)
+            else:
+                w23_codes = [tile("w23_codes0", [P, S], U32)]
+                w23_scales = [tile("w23_scales0", [P, S], U8)]
+                nc.vector.quantize_mx(out=w23_codes[0][:].bitcast(FP8X4), scales=w23_scales[0][:], in_=w23_dealt[0][:])
+            put_rb(t)
+            deal_pair(w23_dealt[t // 2][:, (t % 2) * 2 * S : (t % 2 + 1) * 2 * S], (w3_raw, w2_raw)[t % 2], t // 2, nc.scalar.copy)
 
-        z2_in = tile("z2_in", [P, S, PACK], BF16)
-        nc.vector.tensor_tensor(
-            z2_in[:].rearrange("p (c i) t -> p c t i", i=2),
-            y_gained[:].rearrange("p t (c i) -> p c t i", i=2),
-            gates[:].rearrange("p t (c i) -> p c t i", i=2),
-            MULT,
-        )
-        z_in = tile("z_in", [P, S, PACK], BF16)
-        nc.scalar.copy(
-            z_in[:].rearrange("p (c i) t -> p c t i", i=4), z_planes[:].rearrange("p t (c i) -> p c t i", i=4)
-        )
-        w2_q = [quantise_pair("w2_q0", dealt23["w2", 0])]
-        z2_q = quantise("z2_q", z2_in[:].rearrange("p c t -> p (c t)"), S)
-        z_q = quantise("z_q", z_in[:].rearrange("p c t -> p (c t)"), S)
-        w3_q.append(quantise_pair("w3_q1", dealt23["w3", 1]))
-        w2_q.append(quantise_pair("w2_q1", dealt23["w2", 1]))
+        z2_in = [tile("z2_in%d" % half, [P, HALF, PACK], BF16) for half in range(2)]
+        z_in = [tile("z_in%d" % half, [P, HALF, PACK], BF16) for half in range(2)]
+        for half in range(2):
+            nc.vector.tensor_tensor(
+                z2_in[half][:].rearrange("p (c i) t -> p c t i", i=2),
+                y_gained[:, :, cols(half)].rearrange("p t (c i) -> p c t i", i=2),
+                gates[:, :, cols(half)].rearrange("p t (c i) -> p c t i", i=2),
+                MULT,
+            )
+            nc.scalar.copy(
+                z_in[half][:].rearrange("p (c i) t -> p c t i", i=4),
+                z_planes[:, :, cols(half)].rearrange("p t (c i) -> p c t i", i=4),
+            )
+        z2_codes = tile("z2_codes", [P, S], U32)
+        z2_scales = tile("z2_scales", [P, S], U8)
+        z_codes = tile("z_codes", [P, S], U32)
+        z_scales = tile("z_scales", [P, S], U8)
+        for half in range(2):
+            for src, codes, scales in ((z2_in, z2_codes, z2_scales), (z_in, z_codes, z_scales)):
+                nc.vector.quantize_mx(
+                    out=codes[:, cols(half)].bitcast(FP8X4),
+                    scales=scales[:, cols(half)],
+                    in_=src[half][:].rearrange("p c t -> p (c t)"),
+                )
+        w23_codes.append(tile("w23_codes1", [P, S], U32, tag="z_in1"))
+        w23_scales.append(tile("w23_scales1", [P, S], U8))
+        nc.vector.quantize_mx(out=w23_codes[1][:].bitcast(FP8X4), scales=w23_scales[1][:], in_=w23_dealt[1][:])
 
-        h_banks = [psum.tile([P, S], F32, name="h_bank%d" % t) for t in range(PACK)]
-        for pair in range(2):
-            for t in (2 * pair, 2 * pair + 1):
-                mx_pass(h_banks[t], w3_q[pair], t, z2_q, True, False)
-            for t in (2 * pair, 2 * pair + 1):
-                mx_pass(h_banks[t], w2_q[pair], t, z_q, False, True)
+        h_banks = {}
+        for t in range(PACK):
+            for half in range(2):
+                acc = bank("h", t, half)
+                h_banks[t, half] = acc
+                w_codes, w_scales = w23_codes[t // 2], w23_scales[t // 2]
+                mx_pass(acc, w_codes, w_scales, t % 2, z2_codes, z2_scales, half, True, False)
+                mx_pass(acc, w_codes, w_scales, 2 + t % 2, z_codes, z_scales, half, False, True)
+                nc.scalar.copy(rows[t][:, cols(half)], acc[:])
 
         out_rows = out.rearrange("(p t) c -> p t c", t=PACK)
-        pieces = [(0, 0, S), (1, 0, S), (2, 0, S), (3, 0, HALF), (3, HALF, S)]
-        second = [tile("second%d" % u, [P, b - a], F32) for u, (t, a, b) in enumerate(pieces)]
-        diff = [tile("diff%d" % u, [P, b - a], F32) for u, (t, a, b) in enumerate(pieces)]
-        gate = [tile("gate%d" % u, [P, b - a], F32) for u, (t, a, b) in enumerate(pieces)]
-        result = [tile("result%d" % u, [P, b - a], F32) for u, (t, a, b) in enumerate(pieces)]
+        second = [tile("second%d" % t, [P, S], F32) for t in range(PACK)]
+        diff = [tile("diff%d" % t, [P, S], F32) for t in range(PACK)]
+        gate = [tile("gate%d" % t, [P, S], F32) for t in range(PACK)]
+        result = [tile("result%d" % t, [P, S], F32) for t in range(PACK)]
 
-        def fetch_second(u):
-            t, a, b = pieces[u]
-            nc.vector.tensor_copy(second[u][:], rows[t][:].indirect(n6_t[:, a // 16 : b // 16]))
-
-        def fetch_diff(u):
-            t, a, b = pieces[u]
-            nc.vector.tensor_tensor(diff[u][:], rows[t][:].indirect(n5_t[:, a // 16 : b // 16]), second[u][:], SUB)
-            nc.scalar.activation(gate[u][:], diff[u][:], SIGMOID)
-
-        def finish(u):
-            t, a, b = pieces[u]
-            nc.vector.tensor_tensor(result[u][:], h_banks[t][:, a:b], gate[u][:], MULT)
-            nc.sync.dma_start(out_rows[:, t, a:b], result[u][:])
+        def finish(t, half):
+            if t + 1 < PACK:
+                nc.gpsimd.tensor_tensor(result[t][:, cols(half)], rows[t][:, cols(half)], gate[t][:, cols(half)], MULT)
+            else:
+                nc.vector.tensor_tensor(result[t][:, cols(half)], h_banks[t, half][:], gate[t][:, cols(half)], MULT)
+            nc.sync.dma_start(out_rows[:, t, cols(half)], result[t][:, cols(half)])
 
         for t in range(PACK):
-            nc.scalar.copy(rows[t][:, :S], h_banks[t][:])
-        fetch_second(0)
-        for u in range(len(pieces)):
-            if u + 1 < len(pieces):
-                fetch_second(u + 1)
-            fetch_diff(u)
-            if u > 0:
-                finish(u - 1)
-        finish(len(pieces) - 1)
+            for half in range(2):
+                nc.vector.tensor_copy(second[t][:, cols(half)], rows[t][:].indirect(entries(n6_t, half)))
+            if t > 0:
+                for half in range(2):
+                    finish(t - 1, half)
+            for half in range(2):
+                nc.vector.tensor_tensor(
+                    diff[t][:, cols(half)], rows[t][:].indirect(entries(n5_t, half)), second[t][:, cols(half)], SUB
+                )
+                nc.scalar.activation(gate[t][:, cols(half)], diff[t][:, cols(half)], SIGMOID)
+        for half in range(2):
+            finish(PACK - 1, half)

@@ -78,8 +78,8 @@ def tile_picked_joinhaarhopdcmp_none_p_kernel(
 
         table_scales = tile("table_scales", [P, T], U8)
         nc.vector.memset(table_scales[:].bitcast(I32), 0)
-        three_quarters = tile("three_quarters", [P, HALF], F32)
-        nc.vector.memset(three_quarters[:], 0.75)
+        zero = tile("zero", [P, 1], F32)
+        nc.vector.memset(zero[:], 0.0)
 
         offs_t = load_list("offs_t", offs)
         w1_raw = load_weight("w1_raw", w1)
@@ -90,7 +90,7 @@ def tile_picked_joinhaarhopdcmp_none_p_kernel(
                 table_scales[32 * q : 32 * q + 4, :].bitcast(I32), x_scales[0, 4 * q : 4 * q + 4, :].bitcast(I32)
             )
         warm = tile("warm", [P, 1], F32)
-        nc.scalar.activation(warm[:], three_quarters[:, 0:1], SIGMOID)
+        nc.scalar.activation(warm[:], zero[:], SIGMOID)
         n2_t = load_list("n2_t", n2)
         n1_t = load_list("n1_t", n1)
         n3_t = load_list("n3_t", n3)
@@ -122,90 +122,82 @@ def tile_picked_joinhaarhopdcmp_none_p_kernel(
                 y_banks[t, half] = bank("y", t, half)
                 mx_pass(y_banks[t, half], w1_codes, w1_scales, t, picked_words, picked_scales, half, True, True)
 
+        LAST = PACK - 1
         rows = [tile("rows%d" % t, [P, S], F32) for t in range(PACK)]
         steps = [tile("steps%d" % t, [P, S], F32) for t in range(PACK)]
         y_plain = [tile("y_plain%d" % t, [P, S], F32) for t in range(PACK)]
         y_gained = tile("y_gained", [P, PACK, S], F32)
         gates = tile("gates", [P, PACK, S], F32)
-        z_planes = tile("z_planes", [P, PACK, S], BF16)
+        pa = [tile("pa%d" % t, [P, HALF], F32) for t in range(PACK)]
         pb = [tile("pb%d" % t, [P, HALF], F32) for t in range(PACK)]
-        pb_less = [tile("pb_less%d" % t, [P, HALF], F32) for t in range(PACK)]
-        both = [tile("both%d" % t, [P, HALF], F32) for t in range(PACK)]
         dt = [tile("dt%d" % t, [P, S], F32) for t in range(PACK)]
         w23_dealt = [tile("w23_dealt%d" % pair, [P, 4 * S], BF16) for pair in range(2)]
+        z_in = [tile("z_in%d" % half, [P, HALF, PACK], BF16) for half in range(2)]
 
-        def leave_banks(t):
+        def deal_w23(u):
+            deal_pair(w23_dealt[u // 2][:, (u % 2) * 2 * S : (u % 2 + 1) * 2 * S], (w3_raw, w2_raw)[u % 2], u // 2, nc.scalar.copy)
+
+        for t in range(PACK):
             for half in range(2):
                 nc.scalar.copy(rows[t][:, cols(half)], y_banks[t, half][:])
                 nc.scalar.copy(y_plain[t][:, cols(half)], y_banks[t, half][:])
-
-        def fetch_pb(t):
+            for half in range(2):
+                nc.vector.tensor_tensor(
+                    steps[t][:, cols(half)], rows[t][:].indirect(entries(n3_t, half)), y_plain[t][:, cols(half)], SUB
+                )
+            nc.vector.tensor_copy(pa[t][:], rows[t][:].indirect(n1_t[:]))
             nc.vector.tensor_copy(pb[t][:], rows[t][:].indirect(n2_t[:]))
-            nc.scalar.activation(pb_less[t][:], pb[t][:], COPY, scale=-2.0)
-
-        def fetch_step(t, half):
-            nc.vector.tensor_tensor(
-                steps[t][:, cols(half)], rows[t][:].indirect(entries(n3_t, half)), y_plain[t][:, cols(half)], SUB
-            )
-
-        def fetch_gates(t):
+        for t in range(PACK):
             for half in range(2):
                 nc.scalar.activation(gates[:, t, cols(half)], steps[t][:].indirect(entries(n4_t, half)), SIGMOID)
-            nc.scalar.activation(y_gained[:, t, :], y_plain[t][:], COPY, scale=gm_t[:, t : t + 1])
+            nc.scalar.activation(y_gained[:, t, :], rows[t][:], COPY, scale=gm_t[:, t : t + 1])
 
-        def fetch_both(t):
-            nc.vector.tensor_tensor(both[t][:], rows[t][:].indirect(n1_t[:]), pb[t][:], ADD)
+        pair_values = tile("pair_values", [P, 3 * PACK * HALF], F32, tag="y_plain%d" % LAST)
 
-        def put_ra(t):
-            nc.vector.tensor_tensor(dt[t][:].indirect(n1_t[:]), both[t][:], three_quarters[:], MULT)
+        def pair_value(kind, t):
+            return pair_values[:, (kind * PACK + t) * HALF : (kind * PACK + t + 1) * HALF]
+
+        for t in range(PACK):
+            nc.gpsimd.tensor_tensor(pair_value(0, t), pa[t][:], pb[t][:], SUB)
+            nc.gpsimd.tensor_tensor(pair_value(1, t), pa[t][:], pb[t][:], ADD)
+            deal_w23(t)
+            nc.scalar.activation(pair_value(2, t), pair_value(1, t), COPY, scale=0.75)
 
         def put_rb(t):
-            nc.vector.tensor_tensor(dt[t][:].indirect(n2_t[:]), both[t][:], pb_less[t][:], ADD)
-            nc.scalar.activation(z_planes[:, t, :], dt[t][:], COPY, scale=gn_t[:, t : t + 1])
+            nc.vector.tensor_copy(dt[t][:].indirect(n2_t[:]), pair_value(0, t))
 
-        leave_banks(0)
-        fetch_pb(0)
+        put_rb(0)
         for t in range(PACK):
-            if t + 1 < PACK:
-                leave_banks(t + 1)
-            fetch_step(t, 0)
-            fetch_both(t)
-            fetch_step(t, 1)
-            fetch_gates(t)
-            put_ra(t)
-            if t + 1 < PACK:
-                fetch_pb(t + 1)
-            else:
-                w23_codes = [tile("w23_codes0", [P, S], U32)]
-                w23_scales = [tile("w23_scales0", [P, S], U8)]
-                nc.vector.quantize_mx(out=w23_codes[0][:].bitcast(FP8X4), scales=w23_scales[0][:], in_=w23_dealt[0][:])
-            put_rb(t)
-            deal_pair(w23_dealt[t // 2][:, (t % 2) * 2 * S : (t % 2 + 1) * 2 * S], (w3_raw, w2_raw)[t % 2], t // 2, nc.scalar.copy)
+            if t < LAST:
+                put_rb(t + 1)
+            nc.vector.tensor_copy(dt[t][:].indirect(n1_t[:]), pair_value(2, t))
+            for half in range(2):
+                nc.scalar.activation(z_in[half][:, :, t], dt[t][:, cols(half)], COPY, scale=gn_t[:, t : t + 1])
 
-        z2_in = [tile("z2_in%d" % half, [P, HALF, PACK], BF16) for half in range(2)]
-        z_in = [tile("z_in%d" % half, [P, HALF, PACK], BF16) for half in range(2)]
-        for half in range(2):
-            nc.vector.tensor_tensor(
-                z2_in[half][:].rearrange("p (c i) t -> p c t i", i=2),
-                y_gained[:, :, cols(half)].rearrange("p t (c i) -> p c t i", i=2),
-                gates[:, :, cols(half)].rearrange("p t (c i) -> p c t i", i=2),
-                MULT,
-            )
-            nc.scalar.copy(
-                z_in[half][:].rearrange("p (c i) t -> p c t i", i=4),
-                z_planes[:, :, cols(half)].rearrange("p t (c i) -> p c t i", i=4),
-            )
-        z2_codes = tile("z2_codes", [P, S], U32)
+        z2_in = tile("z2_in", [P, S, PACK], BF16)
+        nc.gpsimd.tensor_tensor(
+            z2_in[:].rearrange("p (c i) t -> p c t i", i=2),
+            y_gained[:].rearrange("p t (c i) -> p c t i", i=2),
+            gates[:].rearrange("p t (c i) -> p c t i", i=2),
+            MULT,
+        )
+        late_codes = tile("late_codes", [P, 2 * S], U32, tag="y_plain%d" % LAST)
+        w23_codes = [late_codes[:, S:]]
+        w23_scales = [tile("w23_scales0", [P, S], U8)]
+        nc.vector.quantize_mx(out=w23_codes[0].bitcast(FP8X4), scales=w23_scales[0][:], in_=w23_dealt[0][:])
+        z2_codes = late_codes[:, :S]
         z2_scales = tile("z2_scales", [P, S], U8)
-        z_codes = tile("z_codes", [P, S], U32)
+        nc.vector.quantize_mx(
+            out=z2_codes.bitcast(FP8X4), scales=z2_scales[:], in_=z2_in[:].rearrange("p c t -> p (c t)")
+        )
+        z_codes = tile("z_codes", [P, S], U32, tag="z2_in")
         z_scales = tile("z_scales", [P, S], U8)
         for half in range(2):
-            for src, codes, scales in ((z2_in, z2_codes, z2_scales), (z_in, z_codes, z_scales)):
-                nc.vector.quantize_mx(
-                    out=codes[:, cols(half)].bitcast(FP8X4),
-                    scales=scales[:, cols(half)],
-                    in_=src[half][:].rearrange("p c t -> p (c t)"),
-                )
+            nc.vector.quantize_mx(
+                out=z_codes[:, cols(half)].bitcast(FP8X4),
+                scales=z_scales[:, cols(half)],
+                in_=z_in[half][:].rearrange("p c t -> p (c t)"),
+            )
         w23_codes.append(tile("w23_codes1", [P, S], U32, tag="z_in1"))
         w23_scales.append(tile("w23_scales1", [P, S], U8))
         nc.vector.quantize_mx(out=w23_codes[1][:].bitcast(FP8X4), scales=w23_scales[1][:], in_=w23_dealt[1][:])
@@ -226,23 +218,36 @@ def tile_picked_joinhaarhopdcmp_none_p_kernel(
         gate = [tile("gate%d" % t, [P, S], F32) for t in range(PACK)]
         result = [tile("result%d" % t, [P, S], F32) for t in range(PACK)]
 
-        def finish(t, half):
-            if t + 1 < PACK:
-                nc.gpsimd.tensor_tensor(result[t][:, cols(half)], rows[t][:, cols(half)], gate[t][:, cols(half)], MULT)
+        def finish(t, first, last):
+            if t < LAST:
+                nc.gpsimd.tensor_tensor(result[t][:, first:last], rows[t][:, first:last], gate[t][:, first:last], MULT)
             else:
-                nc.vector.tensor_tensor(result[t][:, cols(half)], h_banks[t, half][:], gate[t][:, cols(half)], MULT)
-            nc.sync.dma_start(out_rows[:, t, cols(half)], result[t][:, cols(half)])
+                half = first // HALF
+                nc.vector.tensor_tensor(
+                    result[t][:, first:last],
+                    h_banks[t, half][:, first - half * HALF : last - half * HALF],
+                    gate[t][:, first:last],
+                    MULT,
+                )
+            nc.sync.dma_start(out_rows[:, t, first:last], result[t][:, first:last])
+
+        def pieces(t):
+            cuts = (0, HALF, S) if t < LAST else (0, HALF, HALF + P, S)
+            return list(zip(cuts[:-1], cuts[1:]))
 
         for t in range(PACK):
             for half in range(2):
                 nc.vector.tensor_copy(second[t][:, cols(half)], rows[t][:].indirect(entries(n6_t, half)))
             if t > 0:
-                for half in range(2):
-                    finish(t - 1, half)
-            for half in range(2):
+                for first, last in pieces(t - 1):
+                    finish(t - 1, first, last)
+            for first, last in pieces(t):
                 nc.vector.tensor_tensor(
-                    diff[t][:, cols(half)], rows[t][:].indirect(entries(n5_t, half)), second[t][:, cols(half)], SUB
+                    diff[t][:, first:last],
+                    rows[t][:].indirect(n5_t[:, first // 16 : last // 16]),
+                    second[t][:, first:last],
+                    SUB,
                 )
-                nc.scalar.activation(gate[t][:, cols(half)], diff[t][:, cols(half)], SIGMOID)
-        for half in range(2):
-            finish(PACK - 1, half)
+                nc.scalar.activation(gate[t][:, first:last], diff[t][:, first:last], SIGMOID)
+        for first, last in pieces(LAST):
+            finish(LAST, first, last)

@@ -57,7 +57,7 @@ def tile_picked_joinhaarhopdcmp_none_p_kernel(
 
         def deal_pair(dst, raw, pair, copy):
             copy(
-                dst.rearrange("p (t m j) -> p m j t", t=2, j=PACK),
+                dst.rearrange("p t (m j) -> p m j t", j=PACK),
                 raw[:].rearrange("p j (m t) -> p m j t", t=PACK)[:, :, :, 2 * pair : 2 * pair + 2],
             )
 
@@ -78,8 +78,6 @@ def tile_picked_joinhaarhopdcmp_none_p_kernel(
 
         table_scales = tile("table_scales", [P, T], U8)
         nc.vector.memset(table_scales[:].bitcast(I32), 0)
-        zero = tile("zero", [P, 1], F32)
-        nc.vector.memset(zero[:], 0.0)
 
         offs_t = load_list("offs_t", offs)
         w1_raw = load_weight("w1_raw", w1)
@@ -89,8 +87,6 @@ def tile_picked_joinhaarhopdcmp_none_p_kernel(
             nc.scalar.dma_start(
                 table_scales[32 * q : 32 * q + 4, :].bitcast(I32), x_scales[0, 4 * q : 4 * q + 4, :].bitcast(I32)
             )
-        warm = tile("warm", [P, 1], F32)
-        nc.scalar.activation(warm[:], zero[:], SIGMOID)
         n2_t = load_list("n2_t", n2)
         n1_t = load_list("n1_t", n1)
         n3_t = load_list("n3_t", n3)
@@ -107,10 +103,10 @@ def tile_picked_joinhaarhopdcmp_none_p_kernel(
         w1_codes = tile("w1_codes", [P, S], U32)
         w1_scales = tile("w1_scales", [P, S], U8)
         for pair, copy in enumerate((nc.vector.tensor_copy, nc.scalar.copy)):
-            dealt = tile("w1_dealt%d" % pair, [P, 2 * S], BF16)
+            dealt = tile("w1_dealt%d" % pair, [P, 2, S], BF16)
             deal_pair(dealt[:], w1_raw, pair, copy)
             nc.vector.quantize_mx(
-                out=w1_codes[:, cols(pair)].bitcast(FP8X4), scales=w1_scales[:, cols(pair)], in_=dealt[:]
+                out=w1_codes[:, cols(pair)].bitcast(FP8X4), scales=w1_scales[:, cols(pair)], in_=dealt[:].rearrange("p t c -> p (t c)")
             )
         picked_words = tile("picked_words", [P, S], U32)
         for half in range(2):
@@ -124,68 +120,57 @@ def tile_picked_joinhaarhopdcmp_none_p_kernel(
 
         LAST = PACK - 1
         rows = [tile("rows%d" % t, [P, S], F32) for t in range(PACK)]
+        hop = [tile("hop%d" % t, [P, S], F32) for t in range(PACK)]
         steps = [tile("steps%d" % t, [P, S], F32) for t in range(PACK)]
-        y_plain = [tile("y_plain%d" % t, [P, S], F32) for t in range(PACK)]
-        y_gained = tile("y_gained", [P, PACK, S], F32)
-        gates = tile("gates", [P, PACK, S], F32)
+        y_gained = [tile("y_gained%d" % t, [P, S], F32) for t in range(PACK)]
+        gates = [tile("gates%d" % t, [P, S], F32) for t in range(PACK)]
         pa = [tile("pa%d" % t, [P, HALF], F32) for t in range(PACK)]
         pb = [tile("pb%d" % t, [P, HALF], F32) for t in range(PACK)]
+        both = [tile("both%d" % t, [P, HALF], F32) for t in range(PACK)]
+        rb = [tile("rb%d" % t, [P, HALF], F32) for t in range(PACK)]
         dt = [tile("dt%d" % t, [P, S], F32) for t in range(PACK)]
-        w23_dealt = [tile("w23_dealt%d" % pair, [P, 4 * S], BF16) for pair in range(2)]
+        w23_dealt = tile("w23_dealt", [P, PACK, 2, S], BF16)
         z_in = [tile("z_in%d" % half, [P, HALF, PACK], BF16) for half in range(2)]
-
-        def deal_w23(u):
-            deal_pair(w23_dealt[u // 2][:, (u % 2) * 2 * S : (u % 2 + 1) * 2 * S], (w3_raw, w2_raw)[u % 2], u // 2, nc.scalar.copy)
+        z2_planes = tile("z2_planes", [P, PACK, S], BF16)
+        z2_in = tile("z2_in", [P, S, PACK], BF16)
 
         for t in range(PACK):
             for half in range(2):
                 nc.scalar.copy(rows[t][:, cols(half)], y_banks[t, half][:])
-                nc.scalar.copy(y_plain[t][:, cols(half)], y_banks[t, half][:])
+        for t in range(PACK):
             for half in range(2):
-                nc.vector.tensor_tensor(
-                    steps[t][:, cols(half)], rows[t][:].indirect(entries(n3_t, half)), y_plain[t][:, cols(half)], SUB
-                )
+                nc.vector.tensor_copy(hop[t][:, cols(half)], rows[t][:].indirect(entries(n3_t, half)))
             nc.vector.tensor_copy(pa[t][:], rows[t][:].indirect(n1_t[:]))
             nc.vector.tensor_copy(pb[t][:], rows[t][:].indirect(n2_t[:]))
-        for t in range(PACK):
+            nc.gpsimd.tensor_tensor(steps[t][:], hop[t][:], rows[t][:], SUB)
+            nc.gpsimd.tensor_tensor(both[t][:], pa[t][:], pb[t][:], ADD)
+            nc.gpsimd.tensor_tensor(rb[t][:], pa[t][:], pb[t][:], SUB)
+            nc.scalar.activation(y_gained[t][:], rows[t][:], COPY, scale=gm_t[:, t : t + 1])
             for half in range(2):
-                nc.scalar.activation(gates[:, t, cols(half)], steps[t][:].indirect(entries(n4_t, half)), SIGMOID)
-            nc.scalar.activation(y_gained[:, t, :], rows[t][:], COPY, scale=gm_t[:, t : t + 1])
-
-        pair_values = tile("pair_values", [P, 3 * PACK * HALF], F32, tag="y_plain%d" % LAST)
-
-        def pair_value(kind, t):
-            return pair_values[:, (kind * PACK + t) * HALF : (kind * PACK + t + 1) * HALF]
+                nc.scalar.activation(gates[t][:, cols(half)], steps[t][:].indirect(entries(n4_t, half)), SIGMOID)
+        ra_all = tile("ra_all", [P, PACK * HALF], F32, tag="steps%d" % LAST)
+        ra = [ra_all[:, cols(t)] for t in range(PACK)]
+        for t in range(PACK):
+            nc.scalar.activation(ra[t], both[t][:], COPY, scale=0.75)
+        for t in range(PACK):
+            nc.gpsimd.tensor_tensor(z2_planes[:, t, :], y_gained[t][:], gates[t][:], MULT)
+            pair, which = divmod(t, 2)
+            deal_pair(w23_dealt[:, 2 * pair : 2 * pair + 2, which, :], (w3_raw, w2_raw)[which], pair, nc.scalar.copy)
+        nc.gpsimd.tensor_scalar(z2_in[:], z2_planes[:].rearrange("p t c -> p c t"), 1.0, 0.0, MULT, ADD)
 
         for t in range(PACK):
-            nc.gpsimd.tensor_tensor(pair_value(0, t), pa[t][:], pb[t][:], SUB)
-            nc.gpsimd.tensor_tensor(pair_value(1, t), pa[t][:], pb[t][:], ADD)
-            deal_w23(t)
-            nc.scalar.activation(pair_value(2, t), pair_value(1, t), COPY, scale=0.75)
-
-        def put_rb(t):
-            nc.vector.tensor_copy(dt[t][:].indirect(n2_t[:]), pair_value(0, t))
-
-        put_rb(0)
+            nc.vector.tensor_copy(dt[t][:].indirect(n2_t[:]), rb[t][:])
         for t in range(PACK):
-            if t < LAST:
-                put_rb(t + 1)
-            nc.vector.tensor_copy(dt[t][:].indirect(n1_t[:]), pair_value(2, t))
+            nc.vector.tensor_copy(dt[t][:].indirect(n1_t[:]), ra[t])
             for half in range(2):
                 nc.scalar.activation(z_in[half][:, :, t], dt[t][:, cols(half)], COPY, scale=gn_t[:, t : t + 1])
 
-        z2_in = tile("z2_in", [P, S, PACK], BF16)
-        nc.gpsimd.tensor_tensor(
-            z2_in[:].rearrange("p (c i) t -> p c t i", i=2),
-            y_gained[:].rearrange("p t (c i) -> p c t i", i=2),
-            gates[:].rearrange("p t (c i) -> p c t i", i=2),
-            MULT,
-        )
-        late_codes = tile("late_codes", [P, 2 * S], U32, tag="y_plain%d" % LAST)
-        w23_codes = [late_codes[:, S:]]
-        w23_scales = [tile("w23_scales0", [P, S], U8)]
-        nc.vector.quantize_mx(out=w23_codes[0].bitcast(FP8X4), scales=w23_scales[0][:], in_=w23_dealt[0][:])
-        z2_codes = late_codes[:, :S]
+        early_codes = tile("early_codes", [P, S + 2 * P], U32, tag="steps%d" % LAST)
+        first_codes = early_codes[:, S:]
+        z2_codes = early_codes[:, :S]
+        w23_flat = w23_dealt[:].rearrange("p t w c -> p (t w c)")
+        w23_scales = tile("w23_scales", [P, PACK * 2 * P], U8)
+        nc.vector.quantize_mx(out=first_codes.bitcast(FP8X4), scales=w23_scales[:, : 2 * P], in_=w23_flat[:, : 2 * S])
         z2_scales = tile("z2_scales", [P, S], U8)
         nc.vector.quantize_mx(
             out=z2_codes.bitcast(FP8X4), scales=z2_scales[:], in_=z2_in[:].rearrange("p c t -> p (c t)")
@@ -198,18 +183,23 @@ def tile_picked_joinhaarhopdcmp_none_p_kernel(
                 scales=z_scales[:, cols(half)],
                 in_=z_in[half][:].rearrange("p c t -> p (c t)"),
             )
-        w23_codes.append(tile("w23_codes1", [P, S], U32, tag="z_in1"))
-        w23_scales.append(tile("w23_scales1", [P, S], U8))
-        nc.vector.quantize_mx(out=w23_codes[1][:].bitcast(FP8X4), scales=w23_scales[1][:], in_=w23_dealt[1][:])
+        later_codes = tile("later_codes", [P, LAST * 2 * P], U32, tag="z_in1")
+        for first, last in ((1, 2), (2, PACK)):
+            nc.vector.quantize_mx(
+                out=later_codes[:, (first - 1) * 2 * P : (last - 1) * 2 * P].bitcast(FP8X4),
+                scales=w23_scales[:, first * 2 * P : last * 2 * P],
+                in_=w23_flat[:, first * 2 * S : last * 2 * S],
+            )
 
         h_banks = {}
         for t in range(PACK):
             for half in range(2):
                 acc = bank("h", t, half)
                 h_banks[t, half] = acc
-                w_codes, w_scales = w23_codes[t // 2], w23_scales[t // 2]
-                mx_pass(acc, w_codes, w_scales, t % 2, z2_codes, z2_scales, half, True, False)
-                mx_pass(acc, w_codes, w_scales, 2 + t % 2, z_codes, z_scales, half, False, True)
+                w_codes = first_codes if t == 0 else later_codes[:, (t - 1) * 2 * P : t * 2 * P]
+                w_scales = w23_scales[:, t * 2 * P : (t + 1) * 2 * P]
+                mx_pass(acc, w_codes, w_scales, 0, z2_codes, z2_scales, half, True, False)
+                mx_pass(acc, w_codes, w_scales, 1, z_codes, z_scales, half, False, True)
                 nc.scalar.copy(rows[t][:, cols(half)], acc[:])
 
         out_rows = out.rearrange("(p t) c -> p t c", t=PACK)
@@ -219,7 +209,7 @@ def tile_picked_joinhaarhopdcmp_none_p_kernel(
         result = [tile("result%d" % t, [P, S], F32) for t in range(PACK)]
 
         def finish(t, first, last):
-            if t < LAST:
+            if t < LAST and first == 0:
                 nc.gpsimd.tensor_tensor(result[t][:, first:last], rows[t][:, first:last], gate[t][:, first:last], MULT)
             else:
                 half = first // HALF

from contextlib import ExitStack

import concourse.mybir as mybir

F32 = mybir.dt.float32
BF16 = mybir.dt.bfloat16
I32 = mybir.dt.int32
U32 = mybir.dt.uint32
U16 = mybir.dt.uint16
U8 = mybir.dt.uint8
FP8X4 = mybir.dt.float8_e4m3fn_x4
ADD = mybir.AluOpType.add
MULT = mybir.AluOpType.mult
SUB = mybir.AluOpType.subtract
COPY = mybir.ActivationFunctionType.Copy
SIGMOID = mybir.ActivationFunctionType.Sigmoid

P = 128
PACK = 4
T = 2048
S = 512
HALF = 256
FLOPS = 3 * 2 * 512 * 512 * 512


def tile_picked_joinhaarhopdcmp_none_p_kernel(
    tc, x_words, x_scales, w1, gn, gm, w2, w3, offs, n1, n2, n3, n4, n5, n6, out
):
    nc = tc.nc
    with ExitStack() as ctx:
        keep = ctx.enter_context(tc.tile_pool(name="keep", bufs=1))
        psum = ctx.enter_context(tc.psum_pool(name="psum", bufs=1))

        def tile(name, shape, dtype, tag=None):
            return keep.tile(shape, dtype, name=name, tag=tag or name, align_bytes=64)

        def cols(half):
            return slice(half * HALF, (half + 1) * HALF)

        def entries(list_tile, half):
            return list_tile[:, half * (HALF // 16) : (half + 1) * (HALF // 16)]

        def load_list(name, src):
            dst = tile(name, list(src.shape), U16)
            nc.sync.dma_start(dst[:], src)
            return dst

        def load_weight(name, src):
            dst = tile(name, [P, PACK, S], F32)
            nc.sync.dma_start(dst[:], src.rearrange("(p j) c -> p j c", j=PACK))
            return dst

        def load_gain(name, src):
            dst = tile(name, [P, PACK], F32)
            nc.sync.dma_start(dst[:], src.rearrange("(p t) o -> p (t o)", t=PACK))
            return dst

        def deal_pair(dst, raw, pair, copy):
            copy(
                dst.rearrange("p t (m j) -> p m j t", j=PACK),
                raw[:].rearrange("p j (m t) -> p m j t", t=PACK)[:, :, :, 2 * pair : 2 * pair + 2],
            )

        def mx_pass(acc, w_codes, w_scales, block, codes, scales, half, start, stop):
            w_cols = slice(block * P, (block + 1) * P)
            nc.tensor.matmul_mx(
                out=acc[:],
                lhsT=w_codes[:, w_cols].bitcast(FP8X4),
                lhsT_scale=w_scales[:, w_cols],
                rhs=codes[:, cols(half)].bitcast(FP8X4),
                rhs_scale=scales[:, cols(half)],
                start=start,
                stop=stop,
            )

        def bank(name, t, half):
            return psum.tile([P, HALF], F32, name="%s%d_%d" % (name, t, half), tag="bank%d_%d" % (t, half))

        table_scales = tile("table_scales", [P, T], U8)
        nc.vector.memset(table_scales[:].bitcast(I32), 0)

        offs_t = load_list("offs_t", offs)
        w1_raw = load_weight("w1_raw", w1)
        table_words = tile("table_words", [P, T], U32)
        nc.sync.dma_start(table_words[:].bitcast(I32), x_words[0].rearrange("p n t -> p (n t)").bitcast(I32))
        for q in range(4):
            nc.scalar.dma_start(
                table_scales[32 * q : 32 * q + 4, :].bitcast(I32), x_scales[0, 4 * q : 4 * q + 4, :].bitcast(I32)
            )
        n2_t = load_list("n2_t", n2)
        n1_t = load_list("n1_t", n1)
        n3_t = load_list("n3_t", n3)
        n4_t = load_list("n4_t", n4)
        gm_t = load_gain("gm_t", gm)
        gn_t = load_gain("gn_t", gn)
        w3_raw = load_weight("w3_raw", w3)
        w2_raw = load_weight("w2_raw", w2)
        n5_t = load_list("n5_t", n5)
        n6_t = load_list("n6_t", n6)

        picked_scales = tile("picked_scales", [P, S], U8)
        nc.vector.tensor_copy(picked_scales[:], table_scales[:].indirect(offs_t[:]))
        w1_codes = tile("w1_codes", [P, S], U32)
        w1_scales = tile("w1_scales", [P, S], U8)
        for pair, copy in enumerate((nc.vector.tensor_copy, nc.scalar.copy)):
            dealt = tile("w1_dealt%d" % pair, [P, 2, S], BF16)
            deal_pair(dealt[:], w1_raw, pair, copy)
            nc.vector.quantize_mx(
                out=w1_codes[:, cols(pair)].bitcast(FP8X4), scales=w1_scales[:, cols(pair)], in_=dealt[:].rearrange("p t c -> p (t c)")
            )
        picked_words = tile("picked_words", [P, S], U32)
        for half in range(2):
            nc.vector.tensor_copy(picked_words[:, cols(half)], table_words[:].indirect(entries(offs_t, half)))

        y_banks = {}
        for t in range(PACK):
            for half in range(2):
                y_banks[t, half] = bank("y", t, half)
                mx_pass(y_banks[t, half], w1_codes, w1_scales, t, picked_words, picked_scales, half, True, True)

        LAST = PACK - 1
        rows = [tile("rows%d" % t, [P, S], F32) for t in range(PACK)]
        hop = [tile("hop%d" % t, [P, S], F32) for t in range(PACK)]
        steps = [tile("steps%d" % t, [P, S], F32) for t in range(PACK)]
        y_gained = [tile("y_gained%d" % t, [P, S], F32) for t in range(PACK)]
        gates = [tile("gates%d" % t, [P, S], F32) for t in range(PACK)]
        pa = [tile("pa%d" % t, [P, HALF], F32) for t in range(PACK)]
        pb = [tile("pb%d" % t, [P, HALF], F32) for t in range(PACK)]
        both = [tile("both%d" % t, [P, HALF], F32) for t in range(PACK)]
        rb = [tile("rb%d" % t, [P, HALF], F32) for t in range(PACK)]
        dt = [tile("dt%d" % t, [P, S], F32) for t in range(PACK)]
        w23_dealt = tile("w23_dealt", [P, PACK, 2, S], BF16)
        z_in = [tile("z_in%d" % half, [P, HALF, PACK], BF16) for half in range(2)]
        z2_planes = tile("z2_planes", [P, PACK, S], BF16)
        z2_in = tile("z2_in", [P, S, PACK], BF16)

        for t in range(PACK):
            for half in range(2):
                nc.scalar.copy(rows[t][:, cols(half)], y_banks[t, half][:])
        for t in range(PACK):
            for half in range(2):
                nc.vector.tensor_copy(hop[t][:, cols(half)], rows[t][:].indirect(entries(n3_t, half)))
            nc.vector.tensor_copy(pa[t][:], rows[t][:].indirect(n1_t[:]))
            nc.vector.tensor_copy(pb[t][:], rows[t][:].indirect(n2_t[:]))
            nc.gpsimd.tensor_tensor(steps[t][:], hop[t][:], rows[t][:], SUB)
            nc.gpsimd.tensor_tensor(both[t][:], pa[t][:], pb[t][:], ADD)
            nc.gpsimd.tensor_tensor(rb[t][:], pa[t][:], pb[t][:], SUB)
            nc.scalar.activation(y_gained[t][:], rows[t][:], COPY, scale=gm_t[:, t : t + 1])
            for half in range(2):
                nc.scalar.activation(gates[t][:, cols(half)], steps[t][:].indirect(entries(n4_t, half)), SIGMOID)
        ra_all = tile("ra_all", [P, PACK * HALF], F32, tag="steps%d" % LAST)
        ra = [ra_all[:, cols(t)] for t in range(PACK)]
        for t in range(PACK):
            nc.scalar.activation(ra[t], both[t][:], COPY, scale=0.75)
        for t in range(PACK):
            nc.gpsimd.tensor_tensor(z2_planes[:, t, :], y_gained[t][:], gates[t][:], MULT)
            pair, which = divmod(t, 2)
            deal_pair(w23_dealt[:, 2 * pair : 2 * pair + 2, which, :], (w3_raw, w2_raw)[which], pair, nc.scalar.copy)
        nc.gpsimd.tensor_scalar(z2_in[:], z2_planes[:].rearrange("p t c -> p c t"), 1.0, 0.0, MULT, ADD)

        for t in range(PACK):
            nc.vector.tensor_copy(dt[t][:].indirect(n2_t[:]), rb[t][:])
        for t in range(PACK):
            nc.vector.tensor_copy(dt[t][:].indirect(n1_t[:]), ra[t])
            for half in range(2):
                nc.scalar.activation(z_in[half][:, :, t], dt[t][:, cols(half)], COPY, scale=gn_t[:, t : t + 1])

        early_codes = tile("early_codes", [P, S + 2 * P], U32, tag="steps%d" % LAST)
        first_codes = early_codes[:, S:]
        z2_codes = early_codes[:, :S]
        w23_flat = w23_dealt[:].rearrange("p t w c -> p (t w c)")
        w23_scales = tile("w23_scales", [P, PACK * 2 * P], U8)
        nc.vector.quantize_mx(out=first_codes.bitcast(FP8X4), scales=w23_scales[:, : 2 * P], in_=w23_flat[:, : 2 * S])
        z2_scales = tile("z2_scales", [P, S], U8)
        nc.vector.quantize_mx(
            out=z2_codes.bitcast(FP8X4), scales=z2_scales[:], in_=z2_in[:].rearrange("p c t -> p (c t)")
        )
        z_codes = tile("z_codes", [P, S], U32, tag="z2_in")
        z_scales = tile("z_scales", [P, S], U8)
        for half in range(2):
            nc.vector.quantize_mx(
                out=z_codes[:, cols(half)].bitcast(FP8X4),
                scales=z_scales[:, cols(half)],
                in_=z_in[half][:].rearrange("p c t -> p (c t)"),
            )
        later_codes = tile("later_codes", [P, LAST * 2 * P], U32, tag="z_in1")
        for first, last in ((1, 2), (2, PACK)):
            nc.vector.quantize_mx(
                out=later_codes[:, (first - 1) * 2 * P : (last - 1) * 2 * P].bitcast(FP8X4),
                scales=w23_scales[:, first * 2 * P : last * 2 * P],
                in_=w23_flat[:, first * 2 * S : last * 2 * S],
            )

        h_banks = {}
        for t in range(PACK):
            for half in range(2):
                acc = bank("h", t, half)
                h_banks[t, half] = acc
                w_codes = first_codes if t == 0 else later_codes[:, (t - 1) * 2 * P : t * 2 * P]
                w_scales = w23_scales[:, t * 2 * P : (t + 1) * 2 * P]
                mx_pass(acc, w_codes, w_scales, 0, z2_codes, z2_scales, half, True, False)
                mx_pass(acc, w_codes, w_scales, 1, z_codes, z_scales, half, False, True)
                nc.scalar.copy(rows[t][:, cols(half)], acc[:])

        out_rows = out.rearrange("(p t) c -> p t c", t=PACK)
        second = [tile("second%d" % t, [P, S], F32) for t in range(PACK)]
        diff = [tile("diff%d" % t, [P, S], F32) for t in range(PACK)]
        gate = [tile("gate%d" % t, [P, S], F32) for t in range(PACK)]
        result = [tile("result%d" % t, [P, S], F32) for t in range(PACK)]

        def finish(t, first, last):
            if t < LAST and first == 0:
                nc.gpsimd.tensor_tensor(result[t][:, first:last], rows[t][:, first:last], gate[t][:, first:last], MULT)
            else:
                half = first // HALF
                nc.vector.tensor_tensor(
                    result[t][:, first:last],
                    h_banks[t, half][:, first - half * HALF : last - half * HALF],
                    gate[t][:, first:last],
                    MULT,
                )
            nc.sync.dma_start(out_rows[:, t, first:last], result[t][:, first:last])

        def pieces(t):
            cuts = (0, HALF, S) if t < LAST else (0, HALF, HALF + P, S)
            return list(zip(cuts[:-1], cuts[1:]))

        for t in range(PACK):
            for half in range(2):
                nc.vector.tensor_copy(second[t][:, cols(half)], rows[t][:].indirect(entries(n6_t, half)))
            if t > 0:
                for first, last in pieces(t - 1):
                    finish(t - 1, first, last)
            for first, last in pieces(t):
                nc.vector.tensor_tensor(
                    diff[t][:, first:last],
                    rows[t][:].indirect(n5_t[:, first // 16 : last // 16]),
                    second[t][:, first:last],
                    SUB,
                )
                nc.scalar.activation(gate[t][:, first:last], diff[t][:, first:last], SIGMOID)
        for first, last in pieces(LAST):
            finish(LAST, first, last)
